import numpy as np
import ml_dtypes


def mxq(x, axis, fmt="e4m3"):
    dtype, down = {"e4m3": (ml_dtypes.float8_e4m3fn, 7), "e5m2": (ml_dtypes.float8_e5m2, 14)}[fmt]
    v = np.moveaxis(np.asarray(x, np.float32).astype(ml_dtypes.bfloat16).astype(np.float64), axis, -1)
    blocks = v.reshape(v.shape[:-1] + (-1, 32))
    amax = np.abs(blocks).max(-1, keepdims=True)
    byte = np.maximum(np.where(amax > 0, np.frexp(amax)[1] - 1 + 127, 0) - down, 1)
    scale = np.exp2(byte - 127.0)
    codes = (blocks / scale).astype(np.float32).astype(dtype).astype(np.float64)
    return np.moveaxis((codes * scale).reshape(v.shape), -1, axis)


WIDE = False


def mx_kscale(k):
    if not WIDE:
        return np.ones(k)
    levels = np.array([10, -10, 5, -5, 0])
    if k % 512:
        return np.exp2(np.random.permutation(np.resize(levels, k // 32))).repeat(32)
    a = np.empty((k // 512, 16))
    for p in range(k // 512):
        a[p, :8] = np.random.permutation(np.resize(levels, 8))
        for g in range(8):
            far = levels[np.abs(levels - a[p, g]) >= 10]
            a[p, g + 8] = far[np.random.randint(len(far))]
    return np.exp2(a.ravel()).repeat(32)


def f64(x):
    return np.asarray(x).astype(np.float64)


def striped8(idx):
    return np.asarray(idx).reshape(8, -1, 16).transpose(0, 2, 1).reshape(128, -1).astype(np.uint16)


def unstriped8(offs):
    return offs.reshape(8, 16, -1).transpose(0, 2, 1).reshape(8, -1).astype(np.int64)


def pick8(x, idx, run):
    r = np.arange(len(x))
    return x[r[:, None], idx[r % (8 * run) // run]]


E2M1 = np.array([0.0, 0.5, 1.0, 1.5, 2.0, 3.0, 4.0, 6.0, -0.0, -0.5, -1.0, -1.5, -2.0, -3.0, -4.0, -6.0])


def pack_weight(w, fmt):
    k, n = w.shape
    w = f64(np.asarray(w, np.float32).astype(ml_dtypes.bfloat16)).reshape(k // 32, 32, n)
    amax = np.abs(w).max(1)
    if fmt == "e4m3":
        byte = np.frexp(amax)[1] - 1 + 127 - 7
    else:
        mant, ex = np.frexp(amax / 6.0)
        byte = np.where(mant > 0.5, ex, ex - 1) + 127
    byte = np.clip(np.where(amax > 0, byte, 1), 1, 254)
    scaled = (w * np.exp2(127.0 - byte)[:, None, :]).reshape(k, n).astype(np.float32)
    by_word = np.ascontiguousarray(scaled.reshape(k // 512, 128, 4, n).transpose(0, 1, 3, 2))
    if fmt == "e4m3":
        words = by_word.astype(ml_dtypes.float8_e4m3fn).view(np.uint8)
    else:
        c = by_word.astype(ml_dtypes.float4_e2m1fn).view(np.uint8) & 0xF
        words = (c[..., 0::2] | (c[..., 1::2] << 4)).reshape(k // 512, 128, 2 * n)
    return np.ascontiguousarray(words), np.ascontiguousarray(byte.astype(np.uint8).reshape(k // 512, 16, n))


def unpack_weight(words, scales, fmt):
    g, _, n = scales.shape
    words = np.ascontiguousarray(words).reshape(g, 128, n, -1)
    if fmt == "e4m3":
        vals = words.view(ml_dtypes.float8_e4m3fn).astype(np.float64)
    else:
        nib = np.empty((g, 128, n, 4), np.uint8)
        nib[..., 0::2] = words & 0xF
        nib[..., 1::2] = words >> 4
        vals = E2M1[nib]
    vals = vals * np.repeat(np.exp2(scales.astype(np.float64) - 127.0), 8, axis=1)[..., None]
    return vals.transpose(0, 1, 3, 2).reshape(g * 512, n)


D, T, I, Q, E = 512, 1024, 512, 512, 256


def setup_inputs():
    n = np.random.standard_normal
    idx = np.stack([np.random.permutation(T)[:I] for _ in range(8)])
    idx2 = np.stack([np.random.permutation(T)[:I] for _ in range(8)])
    idx3 = np.stack([np.random.permutation(T)[:I] for _ in range(8)])
    idx4 = np.stack([np.random.permutation(T)[:I] for _ in range(8)])
    fd = mx_kscale(D)
    fq = mx_kscale(Q)
    keysp = pack_weight(n((D, T)) / fd[:, None], "e2m1")
    mixp = pack_weight(n((Q, E)) * 1.0 / np.sqrt(Q) / fq[:, None], "e4m3")
    return {
        "query": (n((D, Q)) * 1.0 / np.sqrt(D) * fd[:, None]).astype(np.float32),
        "keys_words": keysp[0],
        "keys_scales": keysp[1],
        "rowf": (np.random.uniform(0.5, 2.0, (Q, 1)) * fq[:, None]).astype(np.float32),
        "mix_words": mixp[0],
        "mix_scales": mixp[1],
        "offs": striped8(idx),
        "offs2": striped8(idx2),
        "offs3": striped8(idx3),
        "offs4": striped8(idx4),
    }


def reference(query, keys_words, keys_scales, rowf, mix_words, mix_scales, offs, offs2, offs3, offs4):
    idx = unstriped8(offs)
    idx2 = unstriped8(offs2)
    idx3 = unstriped8(offs3)
    idx4 = unstriped8(offs4)
    keysu = unpack_weight(keys_words, keys_scales, "e2m1")
    mixu = unpack_weight(mix_words, mix_scales, "e4m3")
    queryq = mxq(f64(query), 0, "e4m3")
    a = queryq.T @ keysu
    f1 = np.zeros((Q, T))
    f1[np.arange(Q)[:, None], idx2[np.arange(Q) % 512 // 64]] = pick8(a, idx, 64)
    c1 = a + f1
    f2 = np.zeros((Q, T))
    f2[np.arange(Q)[:, None], idx[np.arange(Q) % 512 // 64]] = pick8(c1, idx3, 64)
    c2 = c1 - f2
    g = pick8(c2, idx4, 64)
    gw = g * f64(rowf)
    gwq = mxq(gw, 0, "e4m3")
    y = mixu.T @ gwq
    return y

@@ -1,0 +1,190 @@
+from contextlib import ExitStack
+
+import concourse.mybir as mybir
+
+D, T, I, Q, E = 512, 1024, 512, 512, 256
+FLOPS = 2 * D * Q * T + 2 * Q * E * I
+
+F32 = mybir.dt.float32
+BF16 = mybir.dt.bfloat16
+I32 = mybir.dt.int32
+U32 = mybir.dt.uint32
+U16 = mybir.dt.uint16
+U8 = mybir.dt.uint8
+FP8X4 = mybir.dt.float8_e4m3fn_x4
+FP4X4 = mybir.dt.float4_e2m1fn_x4
+COPY = mybir.ActivationFunctionType.Copy
+ADD = mybir.AluOpType.add
+SUB = mybir.AluOpType.subtract
+
+P = 128
+PACK = 4
+BANK = 512
+HALF = I // 2
+LIST_COLS = I // 16
+
+
+def load_scale_rows(nc, plane, rows):
+    for quad in range(4):
+        nc.sync.dma_start(
+            out=plane[32 * quad : 32 * quad + 4, :].bitcast(I32),
+            in_=rows[4 * quad : 4 * quad + 4, :].bitcast(I32),
+        )
+
+
+def tile_attend_loopback_one_mixed_kernel(
+    tc, query, keys_words, keys_scales, rowf, mix_words, mix_scales, offs, offs2, offs3, offs4, out
+):
+    nc = tc.nc
+    with ExitStack() as ctx:
+        lists = ctx.enter_context(tc.tile_pool(name="lists", bufs=1))
+        sb = ctx.enter_context(tc.tile_pool(name="sb", bufs=1))
+        psum = ctx.enter_context(tc.psum_pool(name="psum", bufs=8))
+
+        idx = lists.tile([P, LIST_COLS], U16, name="idx")
+        idx2 = lists.tile([P, LIST_COLS], U16, name="idx2")
+        idx3 = lists.tile([P, LIST_COLS], U16, name="idx3")
+        idx4 = lists.tile([P, LIST_COLS], U16, name="idx4")
+
+        q_raw = sb.tile([P, PACK, Q], F32, name="q_raw")
+        k_words = sb.tile([P, 2 * T], U8, name="k_words", align_bytes=64)
+        k_plane = sb.tile([P, T], U8, name="k_plane", align_bytes=64)
+        m_words = sb.tile([P, E], U32, name="m_words", align_bytes=64)
+        m_plane = sb.tile([P, E], U8, name="m_plane", align_bytes=64)
+        factor = sb.tile([P, PACK], F32, name="factor")
+
+        nc.vector.memset(k_plane[:].bitcast(I32), 0)
+        nc.vector.memset(m_plane[:].bitcast(I32), 0)
+
+        nc.sync.dma_start(out=q_raw[:], in_=query.rearrange("(p j) q -> p j q", j=PACK))
+        load_scale_rows(nc, k_plane, keys_scales[0])
+        nc.sync.dma_start(out=k_words[:].bitcast(I32), in_=keys_words[0].bitcast(I32))
+        nc.sync.dma_start(idx[:], offs)
+        nc.sync.dma_start(idx2[:], offs2)
+        nc.sync.dma_start(idx3[:], offs3)
+        nc.sync.dma_start(idx4[:], offs4)
+        nc.sync.dma_start(out=factor[:], in_=rowf.rearrange("(p t) o -> p (t o)", t=PACK))
+        nc.sync.dma_start(
+            out=m_words[:].bitcast(I32),
+            in_=mix_words[0].rearrange("p e r -> p (e r)").bitcast(I32),
+        )
+        load_scale_rows(nc, m_plane, mix_scales[0])
+
+        f1 = [sb.tile([P, T], F32, name="f1_%d" % b) for b in range(2)]
+        f2 = [sb.tile([P, T], F32, name="f2_%d" % b) for b in range(2)]
+        for window in f1:
+            nc.vector.memset(window[:], 0.0)
+        for window in f2:
+            nc.gpsimd.memset(window[:], 0.0)
+
+        q_by_tile = q_raw[:].rearrange("p j (m t) -> p t m j", t=PACK)
+        q_codes = []
+        q_plane = []
+        for t in range(PACK):
+            grouped = sb.tile([P, P, PACK], BF16, name="q_grouped%d" % t, align_bytes=64)
+            if t == 1:
+                nc.scalar.copy(out=grouped[:], in_=q_by_tile[:, t])
+            else:
+                nc.vector.tensor_copy(out=grouped[:], in_=q_by_tile[:, t])
+            codes = sb.tile([P, P], U32, name="q_codes%d" % t, align_bytes=64)
+            plane = sb.tile([P, P], U8, name="q_plane%d" % t, align_bytes=64)
+            nc.vector.quantize_mx(
+                out=codes[:].bitcast(FP8X4),
+                scales=plane[:],
+                in_=grouped[:].rearrange("p m j -> p (m j)"),
+            )
+            q_codes.append(codes)
+            q_plane.append(plane)
+
+        picked = [sb.tile([P, I], F32, name="picked%d" % b) for b in range(2)]
+        a = [sb.tile([P, T], F32, name="a%d" % t) for t in range(PACK)]
+        c1 = [sb.tile([P, T], F32, name="c1_%d" % t) for t in range(PACK)]
+        c2 = [sb.tile([P, T], F32, name="c2_%d" % t) for t in range(PACK)]
+        half_cols = LIST_COLS // 2
+
+        for t in range(PACK):
+            for b in range(T // BANK):
+                bank = psum.tile([P, BANK], F32, name="bank")
+                nc.tensor.matmul_mx(
+                    out=bank[:],
+                    lhsT=q_codes[t][:].bitcast(FP8X4),
+                    lhsT_scale=q_plane[t][:],
+                    rhs=k_words[:, 2 * BANK * b : 2 * BANK * (b + 1)].bitcast(FP4X4),
+                    rhs_scale=k_plane[:, BANK * b : BANK * (b + 1)],
+                    start=True,
+                    stop=True,
+                )
+                cols = slice(BANK * b, BANK * (b + 1))
+                if t == 0 and b == 0:
+                    nc.vector.tensor_copy(out=a[t][:, cols], in_=bank[:])
+                else:
+                    nc.scalar.copy(out=a[t][:, cols], in_=bank[:])
+            pick = picked[t % 2]
+            if t == 0:
+                nc.vector.tensor_copy(pick[:, :HALF], a[t][:].indirect(idx[:, :half_cols]))
+                nc.scalar.activation(pick[:, HALF:], a[t][:].indirect(idx[:, half_cols:]), COPY)
+            else:
+                nc.scalar.activation(pick[:], a[t][:].indirect(idx[:]), COPY)
+            nc.vector.tensor_copy(f1[t % 2][:].indirect(idx2[:]), pick[:])
+            nc.gpsimd.tensor_tensor(c1[t][:], a[t][:], f1[t % 2][:], ADD)
+
+        gw = sb.tile([P, PACK, I], F32, name="gw")
+        gw_grouped = [
+            sb.tile([P, HALF, PACK], BF16, name="gw_grouped%d" % h, align_bytes=64) for h in range(2)
+        ]
+        for t in range(PACK):
+            pick = picked[t % 2]
+            nc.scalar.activation(pick[:], c1[t][:].indirect(idx3[:]), COPY)
+            nc.vector.tensor_copy(f2[t % 2][:].indirect(idx[:]), pick[:])
+            if t < PACK - 1:
+                nc.gpsimd.tensor_tensor(c2[t][:], c1[t][:], f2[t % 2][:], SUB)
+                nc.scalar.activation(
+                    gw[:, t, :], c2[t][:].indirect(idx4[:]), COPY, scale=factor[:, t : t + 1]
+                )
+            else:
+                nc.vector.tensor_tensor(c2[t][:], c1[t][:], f2[t % 2][:], SUB)
+            if t == 1:
+                for h in range(2):
+                    nc.scalar.copy(
+                        out=gw_grouped[h][:, :, 0:2],
+                        in_=gw[:, 0:2, h * HALF : (h + 1) * HALF].rearrange("p t i -> p i t"),
+                    )
+
+        last = PACK - 1
+        out_view = out.rearrange("(g p) i -> p g i", p=P)
+        for h in range(2):
+            slots = slice(h * HALF, (h + 1) * HALF)
+            nc.scalar.activation(
+                gw[:, last, slots],
+                c2[last][:].indirect(idx4[:, h * half_cols : (h + 1) * half_cols]),
+                COPY,
+                scale=factor[:, last : last + 1],
+            )
+            nc.vector.tensor_copy(
+                out=gw_grouped[h][:, :, 2:4],
+                in_=gw[:, 2:4, slots].rearrange("p t i -> p i t"),
+            )
+            g_codes = sb.tile([P, HALF], U32, name="g_codes%d" % h, align_bytes=64)
+            g_plane = sb.tile([P, HALF], U8, name="g_plane%d" % h, align_bytes=64)
+            nc.vector.quantize_mx(
+                out=g_codes[:].bitcast(FP8X4),
+                scales=g_plane[:],
+                in_=gw_grouped[h][:].rearrange("p i t -> p (i t)"),
+            )
+            result = sb.tile([P, E // P, HALF], F32, name="result%d" % h)
+            for g in range(E // P):
+                bank = psum.tile([P, BANK], F32, name="bank")
+                nc.tensor.matmul_mx(
+                    out=bank[:, :HALF],
+                    lhsT=m_words[:, P * g : P * (g + 1)].bitcast(FP8X4),
+                    lhsT_scale=m_plane[:, P * g : P * (g + 1)],
+                    rhs=g_codes[:].bitcast(FP8X4),
+                    rhs_scale=g_plane[:],
+                    start=True,
+                    stop=True,
+                )
+                if g == 0:
+                    nc.scalar.copy(out=result[:, g, :], in_=bank[:, :HALF])
+                else:
+                    nc.vector.tensor_copy(out=result[:, g, :], in_=bank[:, :HALF])
+            nc.sync.dma_start(out=out_view[:, :, slots], in_=result[:])

@@ -15,12 +15,15 @@ FP8X4 = mybir.dt.float8_e4m3fn_x4
 FP4X4 = mybir.dt.float4_e2m1fn_x4
 COPY = mybir.ActivationFunctionType.Copy
 ADD = mybir.AluOpType.add
+MULT = mybir.AluOpType.mult
 SUB = mybir.AluOpType.subtract
 
 P = 128
 PACK = 4
 BANK = 512
 HALF = I // 2
+PIECE = 128
+PIECES = I // PIECE
 LIST_COLS = I // 16
 
 
@@ -46,19 +49,24 @@ def tile_attend_loopback_one_mixed_kernel(
         idx3 = lists.tile([P, LIST_COLS], U16, name="idx3")
         idx4 = lists.tile([P, LIST_COLS], U16, name="idx4")
 
-        q_raw = sb.tile([P, PACK, Q], F32, name="q_raw")
-        k_words = sb.tile([P, 2 * T], U8, name="k_words", align_bytes=64)
+        q_raw = [sb.tile([P, 2, Q], F32, name="q_raw%d" % u) for u in range(2)]
+        k_words = [sb.tile([P, T], U8, name="k_words%d" % u, align_bytes=64) for u in range(2)]
         k_plane = sb.tile([P, T], U8, name="k_plane", align_bytes=64)
         m_words = sb.tile([P, E], U32, name="m_words", align_bytes=64)
         m_plane = sb.tile([P, E], U8, name="m_plane", align_bytes=64)
         factor = sb.tile([P, PACK], F32, name="factor")
 
-        nc.vector.memset(k_plane[:].bitcast(I32), 0)
+        nc.gpsimd.memset(k_plane[:].bitcast(I32), 0)
         nc.vector.memset(m_plane[:].bitcast(I32), 0)
 
-        nc.sync.dma_start(out=q_raw[:], in_=query.rearrange("(p j) q -> p j q", j=PACK))
+        q_rows = query.rearrange("(p j) q -> p j q", j=PACK)
+        for u in range(2):
+            nc.sync.dma_start(out=q_raw[u][:], in_=q_rows[:, 2 * u : 2 * u + 2, :])
         load_scale_rows(nc, k_plane, keys_scales[0])
-        nc.sync.dma_start(out=k_words[:].bitcast(I32), in_=keys_words[0].bitcast(I32))
+        for u in range(2):
+            nc.sync.dma_start(
+                out=k_words[u][:].bitcast(I32), in_=keys_words[0][:, T * u : T * (u + 1)].bitcast(I32)
+            )
         nc.sync.dma_start(idx[:], offs)
         nc.sync.dma_start(idx2[:], offs2)
         nc.sync.dma_start(idx3[:], offs3)
@@ -77,24 +85,28 @@ def tile_attend_loopback_one_mixed_kernel(
         for window in f2:
             nc.gpsimd.memset(window[:], 0.0)
 
-        q_by_tile = q_raw[:].rearrange("p j (m t) -> p t m j", t=PACK)
-        q_codes = []
-        q_plane = []
-        for t in range(PACK):
-            grouped = sb.tile([P, P, PACK], BF16, name="q_grouped%d" % t, align_bytes=64)
-            if t == 1:
-                nc.scalar.copy(out=grouped[:], in_=q_by_tile[:, t])
+        first = sb.tile([P, P, PACK], BF16, name="q_first", align_bytes=64)
+        rest = sb.tile([P, PACK - 1, P, PACK], BF16, name="q_rest", align_bytes=64)
+        q_codes = sb.tile([P, Q], U32, name="q_codes", align_bytes=64)
+        q_plane = sb.tile([P, Q], U8, name="q_plane", align_bytes=64)
+        rest_view = rest[:].rearrange("p t m j -> p m t j")
+        for u in range(2):
+            raw = q_raw[u][:].rearrange("p j (m t) -> p m t j", t=PACK)
+            nc.vector.tensor_copy(out=first[:, :, 2 * u : 2 * u + 2], in_=raw[:, :, 0, :])
+            if u == 0:
+                nc.vector.tensor_copy(out=rest_view[:, :, :, 0:2], in_=raw[:, :, 1:, :])
             else:
-                nc.vector.tensor_copy(out=grouped[:], in_=q_by_tile[:, t])
-            codes = sb.tile([P, P], U32, name="q_codes%d" % t, align_bytes=64)
-            plane = sb.tile([P, P], U8, name="q_plane%d" % t, align_bytes=64)
-            nc.vector.quantize_mx(
-                out=codes[:].bitcast(FP8X4),
-                scales=plane[:],
-                in_=grouped[:].rearrange("p m j -> p (m j)"),
-            )
-            q_codes.append(codes)
-            q_plane.append(plane)
+                nc.scalar.copy(out=rest_view[:, :, :, 2:4], in_=raw[:, :, 1:, :])
+        nc.vector.quantize_mx(
+            out=q_codes[:, :P].bitcast(FP8X4),
+            scales=q_plane[:, :P],
+            in_=first[:].rearrange("p m j -> p (m j)"),
+        )
+        nc.vector.quantize_mx(
+            out=q_codes[:, P:].bitcast(FP8X4),
+            scales=q_plane[:, P:],
+            in_=rest[:].rearrange("p t m j -> p (t m j)"),
+        )
 
         picked = [sb.tile([P, I], F32, name="picked%d" % b) for b in range(2)]
         a = [sb.tile([P, T], F32, name="a%d" % t) for t in range(PACK)]
@@ -103,22 +115,24 @@ def tile_attend_loopback_one_mixed_kernel(
         half_cols = LIST_COLS // 2
 
         for t in range(PACK):
-            for b in range(T // BANK):
+            width = BANK // 2 if t == 0 else BANK
+            for b in range(T // width):
+                cols = slice(width * b, width * (b + 1))
+                u, c = divmod(width * b, BANK)
                 bank = psum.tile([P, BANK], F32, name="bank")
                 nc.tensor.matmul_mx(
-                    out=bank[:],
-                    lhsT=q_codes[t][:].bitcast(FP8X4),
-                    lhsT_scale=q_plane[t][:],
-                    rhs=k_words[:, 2 * BANK * b : 2 * BANK * (b + 1)].bitcast(FP4X4),
-                    rhs_scale=k_plane[:, BANK * b : BANK * (b + 1)],
+                    out=bank[:, :width],
+                    lhsT=q_codes[:, P * t : P * (t + 1)].bitcast(FP8X4),
+                    lhsT_scale=q_plane[:, P * t : P * (t + 1)],
+                    rhs=k_words[u][:, 2 * c : 2 * (c + width)].bitcast(FP4X4),
+                    rhs_scale=k_plane[:, cols],
                     start=True,
                     stop=True,
                 )
-                cols = slice(BANK * b, BANK * (b + 1))
-                if t == 0 and b == 0:
-                    nc.vector.tensor_copy(out=a[t][:, cols], in_=bank[:])
+                if t == 0 and b % 2 == 0:
+                    nc.vector.tensor_copy(out=a[t][:, cols], in_=bank[:, :width])
                 else:
-                    nc.scalar.copy(out=a[t][:, cols], in_=bank[:])
+                    nc.scalar.copy(out=a[t][:, cols], in_=bank[:, :width])
             pick = picked[t % 2]
             if t == 0:
                 nc.vector.tensor_copy(pick[:, :HALF], a[t][:].indirect(idx[:, :half_cols]))
@@ -128,9 +142,13 @@ def tile_attend_loopback_one_mixed_kernel(
             nc.vector.tensor_copy(f1[t % 2][:].indirect(idx2[:]), pick[:])
             nc.gpsimd.tensor_tensor(c1[t][:], a[t][:], f1[t % 2][:], ADD)
 
+        last = PACK - 1
+        last_factor = sb.tile([P, HALF], F32, name="last_factor", tag="a0")
+        nc.gpsimd.tensor_copy(out=last_factor[:], in_=factor[:, last : last + 1].to_broadcast([P, HALF]))
         gw = sb.tile([P, PACK, I], F32, name="gw")
         gw_grouped = [
-            sb.tile([P, HALF, PACK], BF16, name="gw_grouped%d" % h, align_bytes=64) for h in range(2)
+            sb.tile([P, PIECE, PACK], BF16, name="gw_grouped%d" % n, align_bytes=64)
+            for n in range(PIECES)
         ]
         for t in range(PACK):
             pick = picked[t % 2]
@@ -144,47 +162,52 @@ def tile_attend_loopback_one_mixed_kernel(
             else:
                 nc.vector.tensor_tensor(c2[t][:], c1[t][:], f2[t % 2][:], SUB)
             if t == 1:
-                for h in range(2):
+                for n in range(PIECES):
                     nc.scalar.copy(
-                        out=gw_grouped[h][:, :, 0:2],
-                        in_=gw[:, 0:2, h * HALF : (h + 1) * HALF].rearrange("p t i -> p i t"),
+                        out=gw_grouped[n][:, :, 0:2],
+                        in_=gw[:, 0:2, n * PIECE : (n + 1) * PIECE].rearrange("p t i -> p i t"),
                     )
 
-        last = PACK - 1
         out_view = out.rearrange("(g p) i -> p g i", p=P)
-        for h in range(2):
-            slots = slice(h * HALF, (h + 1) * HALF)
-            nc.scalar.activation(
-                gw[:, last, slots],
-                c2[last][:].indirect(idx4[:, h * half_cols : (h + 1) * half_cols]),
-                COPY,
-                scale=factor[:, last : last + 1],
-            )
-            nc.vector.tensor_copy(
-                out=gw_grouped[h][:, :, 2:4],
-                in_=gw[:, 2:4, slots].rearrange("p t i -> p i t"),
-            )
-            g_codes = sb.tile([P, HALF], U32, name="g_codes%d" % h, align_bytes=64)
-            g_plane = sb.tile([P, HALF], U8, name="g_plane%d" % h, align_bytes=64)
+        nc.vector.tensor_tensor(
+            gw[:, last, :HALF], c2[last][:].indirect(idx4[:, :half_cols]), last_factor[:], MULT
+        )
+        nc.scalar.activation(
+            gw[:, last, HALF:],
+            c2[last][:].indirect(idx4[:, half_cols:]),
+            COPY,
+            scale=factor[:, last : last + 1],
+        )
+        for n in range(PIECES):
+            source = gw[:, 2:4, n * PIECE : (n + 1) * PIECE].rearrange("p t i -> p i t")
+            if n < PIECES // 2:
+                nc.vector.tensor_copy(out=gw_grouped[n][:, :, 2:4], in_=source)
+            else:
+                nc.scalar.copy(out=gw_grouped[n][:, :, 2:4], in_=source)
+        g_codes = [sb.tile([P, PIECE], U32, name="g_codes%d" % n, align_bytes=64) for n in range(PIECES)]
+        g_plane = [sb.tile([P, PIECE], U8, name="g_plane%d" % n, align_bytes=64) for n in range(PIECES)]
+        for n in range(PIECES):
             nc.vector.quantize_mx(
-                out=g_codes[:].bitcast(FP8X4),
-                scales=g_plane[:],
-                in_=gw_grouped[h][:].rearrange("p i t -> p (i t)"),
+                out=g_codes[n][:].bitcast(FP8X4),
+                scales=g_plane[n][:],
+                in_=gw_grouped[n][:].rearrange("p i t -> p (i t)"),
             )
-            result = sb.tile([P, E // P, HALF], F32, name="result%d" % h)
+        for n in range(PIECES):
+            bank = psum.tile([P, BANK], F32, name="bank")
             for g in range(E // P):
-                bank = psum.tile([P, BANK], F32, name="bank")
                 nc.tensor.matmul_mx(
-                    out=bank[:, :HALF],
+                    out=bank[:, PIECE * g : PIECE * (g + 1)],
                     lhsT=m_words[:, P * g : P * (g + 1)].bitcast(FP8X4),
                     lhsT_scale=m_plane[:, P * g : P * (g + 1)],
-                    rhs=g_codes[:].bitcast(FP8X4),
-                    rhs_scale=g_plane[:],
+                    rhs=g_codes[n][:].bitcast(FP8X4),
+                    rhs_scale=g_plane[n][:],
                     start=True,
                     stop=True,
                 )
-                if g == 0:
-                    nc.scalar.copy(out=result[:, g, :], in_=bank[:, :HALF])
-                else:
-                    nc.vector.tensor_copy(out=result[:, g, :], in_=bank[:, :HALF])
-            nc.sync.dma_start(out=out_view[:, :, slots], in_=result[:])
+            result = sb.tile([P, E // P, PIECE], F32, name="result%d" % n)
+            flat = result[:].rearrange("p g i -> p (g i)")
+            if n % 2 == 0:
+                nc.scalar.copy(out=flat, in_=bank[:, : 2 * PIECE])
+            else:
+                nc.vector.tensor_copy(out=flat, in_=bank[:, : 2 * PIECE])
+            nc.sync.dma_start(out=out_view[:, :, n * PIECE : (n + 1) * PIECE], in_=result[:])

@@ -50,23 +50,20 @@ def tile_attend_loopback_one_mixed_kernel(
         idx4 = lists.tile([P, LIST_COLS], U16, name="idx4")
 
         q_raw = [sb.tile([P, 2, Q], F32, name="q_raw%d" % u) for u in range(2)]
-        k_words = [sb.tile([P, T], U8, name="k_words%d" % u, align_bytes=64) for u in range(2)]
+        k_words = sb.tile([P, 2 * T], U8, name="k_words", align_bytes=64)
         k_plane = sb.tile([P, T], U8, name="k_plane", align_bytes=64)
         m_words = sb.tile([P, E], U32, name="m_words", align_bytes=64)
         m_plane = sb.tile([P, E], U8, name="m_plane", align_bytes=64)
         factor = sb.tile([P, PACK], F32, name="factor")
 
         nc.gpsimd.memset(k_plane[:].bitcast(I32), 0)
-        nc.vector.memset(m_plane[:].bitcast(I32), 0)
+        nc.gpsimd.memset(m_plane[:].bitcast(I32), 0)
 
         q_rows = query.rearrange("(p j) q -> p j q", j=PACK)
         for u in range(2):
             nc.sync.dma_start(out=q_raw[u][:], in_=q_rows[:, 2 * u : 2 * u + 2, :])
         load_scale_rows(nc, k_plane, keys_scales[0])
-        for u in range(2):
-            nc.sync.dma_start(
-                out=k_words[u][:].bitcast(I32), in_=keys_words[0][:, T * u : T * (u + 1)].bitcast(I32)
-            )
+        nc.sync.dma_start(out=k_words[:].bitcast(I32), in_=keys_words[0].bitcast(I32))
         nc.sync.dma_start(idx[:], offs)
         nc.sync.dma_start(idx2[:], offs2)
         nc.sync.dma_start(idx3[:], offs3)
@@ -79,11 +76,8 @@ def tile_attend_loopback_one_mixed_kernel(
         load_scale_rows(nc, m_plane, mix_scales[0])
 
         f1 = [sb.tile([P, T], F32, name="f1_%d" % b) for b in range(2)]
-        f2 = [sb.tile([P, T], F32, name="f2_%d" % b) for b in range(2)]
         for window in f1:
             nc.vector.memset(window[:], 0.0)
-        for window in f2:
-            nc.gpsimd.memset(window[:], 0.0)
 
         first = sb.tile([P, P, PACK], BF16, name="q_first", align_bytes=64)
         rest = sb.tile([P, PACK - 1, P, PACK], BF16, name="q_rest", align_bytes=64)
@@ -118,13 +112,12 @@ def tile_attend_loopback_one_mixed_kernel(
             width = BANK // 2 if t == 0 else BANK
             for b in range(T // width):
                 cols = slice(width * b, width * (b + 1))
-                u, c = divmod(width * b, BANK)
                 bank = psum.tile([P, BANK], F32, name="bank")
                 nc.tensor.matmul_mx(
                     out=bank[:, :width],
                     lhsT=q_codes[:, P * t : P * (t + 1)].bitcast(FP8X4),
                     lhsT_scale=q_plane[:, P * t : P * (t + 1)],
-                    rhs=k_words[u][:, 2 * c : 2 * (c + width)].bitcast(FP4X4),
+                    rhs=k_words[:, 2 * width * b : 2 * width * (b + 1)].bitcast(FP4X4),
                     rhs_scale=k_plane[:, cols],
                     start=True,
                     stop=True,
@@ -143,8 +136,13 @@ def tile_attend_loopback_one_mixed_kernel(
             nc.gpsimd.tensor_tensor(c1[t][:], a[t][:], f1[t % 2][:], ADD)
 
         last = PACK - 1
-        last_factor = sb.tile([P, HALF], F32, name="last_factor", tag="a0")
-        nc.gpsimd.tensor_copy(out=last_factor[:], in_=factor[:, last : last + 1].to_broadcast([P, HALF]))
+        f2 = [sb.tile([P, T], F32, name="f2_%d" % b, tag="a%d" % b) for b in range(2)]
+        for window in f2:
+            nc.gpsimd.memset(window[:], 0.0)
+        last_factor = sb.tile([P, HALF], F32, name="last_factor", tag="a2")
+        nc.gpsimd.tensor_scalar(
+            last_factor[:], factor[:, last : last + 1].to_broadcast([P, HALF]), 1.0, 0.0, MULT, ADD
+        )
         gw = sb.tile([P, PACK, I], F32, name="gw")
         gw_grouped = [
             sb.tile([P, PIECE, PACK], BF16, name="gw_grouped%d" % n, align_bytes=64)

from contextlib import ExitStack

import concourse.mybir as mybir

D, T, I, Q, E = 512, 1024, 512, 512, 256
FLOPS = 2 * D * Q * T + 2 * Q * E * I

F32 = mybir.dt.float32
BF16 = mybir.dt.bfloat16
I32 = mybir.dt.int32
U32 = mybir.dt.uint32
U16 = mybir.dt.uint16
U8 = mybir.dt.uint8
FP8X4 = mybir.dt.float8_e4m3fn_x4
FP4X4 = mybir.dt.float4_e2m1fn_x4
COPY = mybir.ActivationFunctionType.Copy
ADD = mybir.AluOpType.add
MULT = mybir.AluOpType.mult
SUB = mybir.AluOpType.subtract

P = 128
PACK = 4
BANK = 512
HALF = I // 2
PIECE = 128
PIECES = I // PIECE
LIST_COLS = I // 16


def load_scale_rows(nc, plane, rows):
    for quad in range(4):
        nc.sync.dma_start(
            out=plane[32 * quad : 32 * quad + 4, :].bitcast(I32),
            in_=rows[4 * quad : 4 * quad + 4, :].bitcast(I32),
        )


def tile_attend_loopback_one_mixed_kernel(
    tc, query, keys_words, keys_scales, rowf, mix_words, mix_scales, offs, offs2, offs3, offs4, out
):
    nc = tc.nc
    with ExitStack() as ctx:
        lists = ctx.enter_context(tc.tile_pool(name="lists", bufs=1))
        sb = ctx.enter_context(tc.tile_pool(name="sb", bufs=1))
        psum = ctx.enter_context(tc.psum_pool(name="psum", bufs=8))

        idx = lists.tile([P, LIST_COLS], U16, name="idx")
        idx2 = lists.tile([P, LIST_COLS], U16, name="idx2")
        idx3 = lists.tile([P, LIST_COLS], U16, name="idx3")
        idx4 = lists.tile([P, LIST_COLS], U16, name="idx4")

        q_raw = [sb.tile([P, 2, Q], F32, name="q_raw%d" % u) for u in range(2)]
        k_words = sb.tile([P, 2 * T], U8, name="k_words", align_bytes=64)
        k_plane = sb.tile([P, T], U8, name="k_plane", align_bytes=64)
        m_words = sb.tile([P, E], U32, name="m_words", align_bytes=64)
        m_plane = sb.tile([P, E], U8, name="m_plane", align_bytes=64)
        factor = sb.tile([P, PACK], F32, name="factor")

        nc.gpsimd.memset(k_plane[:].bitcast(I32), 0)
        nc.gpsimd.memset(m_plane[:].bitcast(I32), 0)

        q_rows = query.rearrange("(p j) q -> p j q", j=PACK)
        for u in range(2):
            nc.sync.dma_start(out=q_raw[u][:], in_=q_rows[:, 2 * u : 2 * u + 2, :])
        load_scale_rows(nc, k_plane, keys_scales[0])
        nc.sync.dma_start(out=k_words[:].bitcast(I32), in_=keys_words[0].bitcast(I32))
        nc.sync.dma_start(idx[:], offs)
        nc.sync.dma_start(idx2[:], offs2)
        nc.sync.dma_start(idx3[:], offs3)
        nc.sync.dma_start(idx4[:], offs4)
        nc.sync.dma_start(out=factor[:], in_=rowf.rearrange("(p t) o -> p (t o)", t=PACK))
        nc.sync.dma_start(
            out=m_words[:].bitcast(I32),
            in_=mix_words[0].rearrange("p e r -> p (e r)").bitcast(I32),
        )
        load_scale_rows(nc, m_plane, mix_scales[0])

        f1 = [sb.tile([P, T], F32, name="f1_%d" % b) for b in range(2)]
        for window in f1:
            nc.vector.memset(window[:], 0.0)

        first = sb.tile([P, P, PACK], BF16, name="q_first", align_bytes=64)
        rest = sb.tile([P, PACK - 1, P, PACK], BF16, name="q_rest", align_bytes=64)
        q_codes = sb.tile([P, Q], U32, name="q_codes", align_bytes=64)
        q_plane = sb.tile([P, Q], U8, name="q_plane", align_bytes=64)
        rest_view = rest[:].rearrange("p t m j -> p m t j")
        for u in range(2):
            raw = q_raw[u][:].rearrange("p j (m t) -> p m t j", t=PACK)
            nc.vector.tensor_copy(out=first[:, :, 2 * u : 2 * u + 2], in_=raw[:, :, 0, :])
            if u == 0:
                nc.vector.tensor_copy(out=rest_view[:, :, :, 0:2], in_=raw[:, :, 1:, :])
            else:
                nc.scalar.copy(out=rest_view[:, :, :, 2:4], in_=raw[:, :, 1:, :])
        nc.vector.quantize_mx(
            out=q_codes[:, :P].bitcast(FP8X4),
            scales=q_plane[:, :P],
            in_=first[:].rearrange("p m j -> p (m j)"),
        )
        nc.vector.quantize_mx(
            out=q_codes[:, P:].bitcast(FP8X4),
            scales=q_plane[:, P:],
            in_=rest[:].rearrange("p t m j -> p (t m j)"),
        )

        picked = [sb.tile([P, I], F32, name="picked%d" % b) for b in range(2)]
        a = [sb.tile([P, T], F32, name="a%d" % t) for t in range(PACK)]
        c1 = [sb.tile([P, T], F32, name="c1_%d" % t) for t in range(PACK)]
        c2 = [sb.tile([P, T], F32, name="c2_%d" % t) for t in range(PACK)]
        half_cols = LIST_COLS // 2

        for t in range(PACK):
            width = BANK // 2 if t == 0 else BANK
            for b in range(T // width):
                cols = slice(width * b, width * (b + 1))
                bank = psum.tile([P, BANK], F32, name="bank")
                nc.tensor.matmul_mx(
                    out=bank[:, :width],
                    lhsT=q_codes[:, P * t : P * (t + 1)].bitcast(FP8X4),
                    lhsT_scale=q_plane[:, P * t : P * (t + 1)],
                    rhs=k_words[:, 2 * width * b : 2 * width * (b + 1)].bitcast(FP4X4),
                    rhs_scale=k_plane[:, cols],
                    start=True,
                    stop=True,
                )
                if t == 0 and b % 2 == 0:
                    nc.vector.tensor_copy(out=a[t][:, cols], in_=bank[:, :width])
                else:
                    nc.scalar.copy(out=a[t][:, cols], in_=bank[:, :width])
            pick = picked[t % 2]
            if t == 0:
                nc.vector.tensor_copy(pick[:, :HALF], a[t][:].indirect(idx[:, :half_cols]))
                nc.scalar.activation(pick[:, HALF:], a[t][:].indirect(idx[:, half_cols:]), COPY)
            else:
                nc.scalar.activation(pick[:], a[t][:].indirect(idx[:]), COPY)
            nc.vector.tensor_copy(f1[t % 2][:].indirect(idx2[:]), pick[:])
            nc.gpsimd.tensor_tensor(c1[t][:], a[t][:], f1[t % 2][:], ADD)

        last = PACK - 1
        f2 = [sb.tile([P, T], F32, name="f2_%d" % b, tag="a%d" % b) for b in range(2)]
        for window in f2:
            nc.gpsimd.memset(window[:], 0.0)
        last_factor = sb.tile([P, HALF], F32, name="last_factor", tag="a2")
        nc.gpsimd.tensor_scalar(
            last_factor[:], factor[:, last : last + 1].to_broadcast([P, HALF]), 1.0, 0.0, MULT, ADD
        )
        gw = sb.tile([P, PACK, I], F32, name="gw")
        gw_grouped = [
            sb.tile([P, PIECE, PACK], BF16, name="gw_grouped%d" % n, align_bytes=64)
            for n in range(PIECES)
        ]
        for t in range(PACK):
            pick = picked[t % 2]
            nc.scalar.activation(pick[:], c1[t][:].indirect(idx3[:]), COPY)
            nc.vector.tensor_copy(f2[t % 2][:].indirect(idx[:]), pick[:])
            if t < PACK - 1:
                nc.gpsimd.tensor_tensor(c2[t][:], c1[t][:], f2[t % 2][:], SUB)
                nc.scalar.activation(
                    gw[:, t, :], c2[t][:].indirect(idx4[:]), COPY, scale=factor[:, t : t + 1]
                )
            else:
                nc.vector.tensor_tensor(c2[t][:], c1[t][:], f2[t % 2][:], SUB)
            if t == 1:
                for n in range(PIECES):
                    nc.scalar.copy(
                        out=gw_grouped[n][:, :, 0:2],
                        in_=gw[:, 0:2, n * PIECE : (n + 1) * PIECE].rearrange("p t i -> p i t"),
                    )

        out_view = out.rearrange("(g p) i -> p g i", p=P)
        nc.vector.tensor_tensor(
            gw[:, last, :HALF], c2[last][:].indirect(idx4[:, :half_cols]), last_factor[:], MULT
        )
        nc.scalar.activation(
            gw[:, last, HALF:],
            c2[last][:].indirect(idx4[:, half_cols:]),
            COPY,
            scale=factor[:, last : last + 1],
        )
        for n in range(PIECES):
            source = gw[:, 2:4, n * PIECE : (n + 1) * PIECE].rearrange("p t i -> p i t")
            if n < PIECES // 2:
                nc.vector.tensor_copy(out=gw_grouped[n][:, :, 2:4], in_=source)
            else:
                nc.scalar.copy(out=gw_grouped[n][:, :, 2:4], in_=source)
        g_codes = [sb.tile([P, PIECE], U32, name="g_codes%d" % n, align_bytes=64) for n in range(PIECES)]
        g_plane = [sb.tile([P, PIECE], U8, name="g_plane%d" % n, align_bytes=64) for n in range(PIECES)]
        for n in range(PIECES):
            nc.vector.quantize_mx(
                out=g_codes[n][:].bitcast(FP8X4),
                scales=g_plane[n][:],
                in_=gw_grouped[n][:].rearrange("p i t -> p (i t)"),
            )
        for n in range(PIECES):
            bank = psum.tile([P, BANK], F32, name="bank")
            for g in range(E // P):
                nc.tensor.matmul_mx(
                    out=bank[:, PIECE * g : PIECE * (g + 1)],
                    lhsT=m_words[:, P * g : P * (g + 1)].bitcast(FP8X4),
                    lhsT_scale=m_plane[:, P * g : P * (g + 1)],
                    rhs=g_codes[n][:].bitcast(FP8X4),
                    rhs_scale=g_plane[n][:],
                    start=True,
                    stop=True,
                )
            result = sb.tile([P, E // P, PIECE], F32, name="result%d" % n)
            flat = result[:].rearrange("p g i -> p (g i)")
            if n % 2 == 0:
                nc.scalar.copy(out=flat, in_=bank[:, : 2 * PIECE])
            else:
                nc.vector.tensor_copy(out=flat, in_=bank[:, : 2 * PIECE])
            nc.sync.dma_start(out=out_view[:, :, n * PIECE : (n + 1) * PIECE], in_=result[:])
